import numpy as np
import ml_dtypes


def mxq(x, axis, fmt="e4m3"):
    dtype, down = {"e4m3": (ml_dtypes.float8_e4m3fn, 7), "e5m2": (ml_dtypes.float8_e5m2, 14)}[fmt]
    v = np.moveaxis(np.asarray(x, np.float32).astype(ml_dtypes.bfloat16).astype(np.float64), axis, -1)
    blocks = v.reshape(v.shape[:-1] + (-1, 32))
    amax = np.abs(blocks).max(-1, keepdims=True)
    byte = np.maximum(np.where(amax > 0, np.frexp(amax)[1] - 1 + 127, 0) - down, 1)
    scale = np.exp2(byte - 127.0)
    codes = (blocks / scale).astype(np.float32).astype(dtype).astype(np.float64)
    return np.moveaxis((codes * scale).reshape(v.shape), -1, axis)


WIDE = False


def mx_kscale(k):
    if not WIDE:
        return np.ones(k)
    levels = np.array([10, -10, 5, -5, 0])
    if k % 512:
        return np.exp2(np.random.permutation(np.resize(levels, k // 32))).repeat(32)
    a = np.empty((k // 512, 16))
    for p in range(k // 512):
        a[p, :8] = np.random.permutation(np.resize(levels, 8))
        for g in range(8):
            far = levels[np.abs(levels - a[p, g]) >= 10]
            a[p, g + 8] = far[np.random.randint(len(far))]
    return np.exp2(a.ravel()).repeat(32)


def f64(x):
    return np.asarray(x).astype(np.float64)


def striped(idx):
    return np.tile(idx.reshape(-1, 16).T, (8, 1)).astype(np.uint16)


def unstriped(offs):
    return offs[:16].T.reshape(-1).astype(np.int64)


E2M1 = np.array([0.0, 0.5, 1.0, 1.5, 2.0, 3.0, 4.0, 6.0, -0.0, -0.5, -1.0, -1.5, -2.0, -3.0, -4.0, -6.0])


def pack_weight(w, fmt):
    k, n = w.shape
    w = f64(np.asarray(w, np.float32).astype(ml_dtypes.bfloat16)).reshape(k // 32, 32, n)
    amax = np.abs(w).max(1)
    if fmt == "e4m3":
        byte = np.frexp(amax)[1] - 1 + 127 - 7
    else:
        mant, ex = np.frexp(amax / 6.0)
        byte = np.where(mant > 0.5, ex, ex - 1) + 127
    byte = np.clip(np.where(amax > 0, byte, 1), 1, 254)
    scaled = (w * np.exp2(127.0 - byte)[:, None, :]).reshape(k, n).astype(np.float32)
    by_word = np.ascontiguousarray(scaled.reshape(k // 512, 128, 4, n).transpose(0, 1, 3, 2))
    if fmt == "e4m3":
        words = by_word.astype(ml_dtypes.float8_e4m3fn).view(np.uint8)
    else:
        c = by_word.astype(ml_dtypes.float4_e2m1fn).view(np.uint8) & 0xF
        words = (c[..., 0::2] | (c[..., 1::2] << 4)).reshape(k // 512, 128, 2 * n)
    return np.ascontiguousarray(words), np.ascontiguousarray(byte.astype(np.uint8).reshape(k // 512, 16, n))


def unpack_weight(words, scales, fmt):
    g, _, n = scales.shape
    words = np.ascontiguousarray(words).reshape(g, 128, n, -1)
    if fmt == "e4m3":
        vals = words.view(ml_dtypes.float8_e4m3fn).astype(np.float64)
    else:
        nib = np.empty((g, 128, n, 4), np.uint8)
        nib[..., 0::2] = words & 0xF
        nib[..., 1::2] = words >> 4
        vals = E2M1[nib]
    vals = vals * np.repeat(np.exp2(scales.astype(np.float64) - 127.0), 8, axis=1)[..., None]
    return vals.transpose(0, 1, 3, 2).reshape(g * 512, n)


def relu(v):
    return np.maximum(v, 0.0)


K, T, E, C, H, N = 512, 1280, 8, 256, 512, 384


def by_expert(wq, xq):
    return np.concatenate([wq[e].T @ xq[:, e * C:(e + 1) * C] for e in range(E)], axis=1)


def setup_inputs():
    n = np.random.standard_normal
    s = mx_kscale(K)[:, None]
    u = mx_kscale(H)
    w1 = [pack_weight(m, "e2m1") for m in n((E, K, H)) / np.sqrt(K) / s[None]]
    w3 = [pack_weight(m, "e2m1") for m in n((E, K, H)) / np.sqrt(K) / s[None] * u[None, None, :]]
    w2 = [pack_weight(m, "e2m1") for m in n((E, H, N)) / np.sqrt(H) / u[None, :, None]]
    idx = np.random.permutation(E * C)
    return {
        "xT": (n((K, T)) * s).astype(np.float32),
        "w1_words": np.stack([m[0] for m in w1]),
        "w1_scales": np.stack([m[1] for m in w1]),
        "w3_words": np.stack([m[0] for m in w3]),
        "w3_scales": np.stack([m[1] for m in w3]),
        "w2_words": np.stack([m[0] for m in w2]),
        "w2_scales": np.stack([m[1] for m in w2]),
        "gate": np.tile(np.where(idx < T, np.random.uniform(0.2, 1.0, E * C), 0.0), (N, 1)).astype(np.float32),
        "offs": striped(idx),
    }


def reference(xT, w1_words, w1_scales, w3_words, w3_scales, w2_words, w2_scales, gate, offs):
    idx = unstriped(offs)
    w1 = np.stack([unpack_weight(w1_words[e], w1_scales[e], "e2m1") for e in range(E)])
    w3 = np.stack([unpack_weight(w3_words[e], w3_scales[e], "e2m1") for e in range(E)])
    w2 = np.stack([unpack_weight(w2_words[e], w2_scales[e], "e2m1") for e in range(E)])
    xq = mxq(np.concatenate([f64(xT), np.zeros((K, E * C - T))], axis=1)[:, idx], 0, "e4m3")
    h = relu(by_expert(w1, xq))
    h = h * by_expert(w3, xq)
    y = by_expert(w2, mxq(h, 0, "e4m3"))
    out = np.zeros((N, E * C))
    out[:, idx] = f64(gate) * y
    return out[:, :T]

@@ -1,0 +1,167 @@
+from contextlib import ExitStack
+
+import concourse.mybir as mybir
+from concourse.masks import make_identity
+
+K, T, E, C, H, N = 512, 1280, 8, 256, 512, 384
+S = E * C
+P = 128
+PACK = 4
+FLOPS = 2 * S * (2 * K * H + H * N)
+
+F32 = mybir.dt.float32
+BF16 = mybir.dt.bfloat16
+I32 = mybir.dt.int32
+U32 = mybir.dt.uint32
+U16 = mybir.dt.uint16
+U8 = mybir.dt.uint8
+FP8X4 = mybir.dt.float8_e4m3fn_x4
+FP4X4 = mybir.dt.float4_e2m1fn_x4
+MULT = mybir.AluOpType.mult
+RELU = mybir.ActivationFunctionType.Relu
+
+X_CHUNKS = (256, 256, 256, 256, 128, 128)
+ROW_BLOCKS = N // P
+PAIRS = E // 2
+
+
+def tile_moe_pad_glu_relu_kernel(
+    tc, xT, w1_words, w1_scales, w3_words, w3_scales, w2_words, w2_scales, gate, offs, out
+):
+    nc = tc.nc
+    with ExitStack() as ctx:
+        keep = ctx.enter_context(tc.tile_pool(name="keep", bufs=1))
+        work = ctx.enter_context(tc.tile_pool(name="work", bufs=3))
+        psum = ctx.enter_context(tc.psum_pool(name="psum", bufs=2))
+
+        offsets = keep.tile([P, S // 16], U16, name="offsets")
+        x_raw = [keep.tile([P, PACK, w], F32, name="x_raw%d" % i) for i, w in enumerate(X_CHUNKS)]
+        starts = [sum(X_CHUNKS[:i]) for i in range(len(X_CHUNKS))]
+        x_rows = xT.rearrange("(p j) t -> p j t", j=PACK)
+        for raw, t0, w in zip(x_raw, starts, X_CHUNKS):
+            nc.sync.dma_start(out=raw[:], in_=x_rows[:, :, t0 : t0 + w])
+        nc.sync.dma_start(offsets[:], offs)
+
+        tok_words = keep.tile([P, S], I32, name="tok_words", align_bytes=64)
+        tok_scales = keep.tile([P, S], U8, name="tok_scales", align_bytes=64)
+        nc.gpsimd.memset(tok_scales[:], 0)
+        nc.vector.memset(tok_words[:, T:], 0)
+        ident = keep.tile([P, P], F32, name="ident")
+        make_identity(nc, ident[:])
+
+        def scale_plane(name, width):
+            plane = keep.tile([P, E, width], U8, name=name, align_bytes=64)
+            nc.vector.memset(plane[:].bitcast(I32), 0)
+            return plane
+
+        def load_plane(plane, scales):
+            for q in range(4):
+                nc.sync.dma_start(
+                    out=plane[32 * q : 32 * q + 4, :, :].bitcast(I32),
+                    in_=scales[:, 0, 4 * q : 4 * q + 4, :].rearrange("e r n -> r e n").bitcast(I32),
+                )
+
+        def load_words(name, words, pair):
+            width = words.shape[3]
+            tile = keep.tile([P, 2, width], U8, name="%s_%d" % (name, pair), align_bytes=64)
+            nc.sync.dma_start(
+                out=tile[:].bitcast(I32),
+                in_=words[2 * pair : 2 * pair + 2, 0].rearrange("e p n -> p e n").bitcast(I32),
+            )
+            return tile
+
+        s1 = scale_plane("s1", H)
+        s3 = scale_plane("s3", H)
+        s2 = scale_plane("s2", N)
+        load_plane(s1, w1_scales)
+        load_plane(s3, w3_scales)
+        load_plane(s2, w2_scales)
+        w1, w3, w2, gates = [], [], [], {}
+        for pair in range(PAIRS):
+            w1.append(load_words("w1", w1_words, pair))
+            w3.append(load_words("w3", w3_words, pair))
+            w2.append(load_words("w2", w2_words, pair))
+        for r in range(ROW_BLOCKS):
+            for half in range(2):
+                g = keep.tile([P, S // 2], F32, name="gate_%d_%d" % (r, half))
+                nc.sync.dma_start(
+                    out=g[:], in_=gate[r * P : (r + 1) * P, half * (S // 2) : (half + 1) * (S // 2)]
+                )
+                gates[r, half] = g
+
+        for i, (raw, t0, w) in enumerate(zip(x_raw, starts, X_CHUNKS)):
+            x_bf = keep.tile([P, w, PACK], BF16, name="x_bf%d" % i, align_bytes=64)
+            nc.vector.tensor_copy(out=x_bf[:], in_=raw[:].rearrange("p j t -> p t j"))
+            nc.vector.quantize_mx(
+                out=tok_words[:, t0 : t0 + w].bitcast(FP8X4),
+                scales=tok_scales[:, t0 : t0 + w],
+                in_=x_bf[:].rearrange("p t j -> p (t j)"),
+            )
+
+        y_pairs = [keep.tile([P, ROW_BLOCKS, 2, C], F32, name="y_%d" % i) for i in range(PAIRS)]
+        for e in range(E):
+            pair, side = divmod(e, 2)
+            slot_offsets = offsets[:, e * (C // 16) : (e + 1) * (C // 16)]
+            slot_words = keep.tile([P, C], U32, name="slot_words%d" % e, align_bytes=64)
+            slot_scales = keep.tile([P, C], U8, name="slot_scales%d" % e, align_bytes=64)
+            nc.vector.tensor_copy(slot_words[:], tok_words[:].bitcast(U32).indirect(slot_offsets))
+            nc.vector.tensor_copy(slot_scales[:], tok_scales[:].indirect(slot_offsets))
+
+            h_turned = psum.tile([P, 2, 2, P], F32, name="h_turned")
+            for st in range(2):
+                cols = slice(st * P, (st + 1) * P)
+                a = psum.tile([P, H], F32, name="a")
+                b = psum.tile([P, H], F32, name="b")
+                for acc, w, s in ((a, w1, s1), (b, w3, s3)):
+                    nc.tensor.matmul_mx(
+                        out=acc[:],
+                        lhsT=slot_words[:, cols].bitcast(FP8X4),
+                        lhsT_scale=slot_scales[:, cols],
+                        rhs=w[pair][:, side, :].bitcast(FP4X4),
+                        rhs_scale=s[:, e, :],
+                        start=True,
+                        stop=True,
+                    )
+                relu_a = work.tile([P, 2, P, 2], F32, name="relu_a")
+                nc.scalar.activation(relu_a[:], a[:].rearrange("s (p u d) -> s u p d", u=2, d=2), RELU)
+                h = work.tile([P, 2, P, 2], BF16, name="h")
+                nc.vector.tensor_tensor(
+                    h[:], b[:].rearrange("s (p u d) -> s u p d", u=2, d=2), relu_a[:], MULT
+                )
+                h_words = h[:].rearrange("s u p d -> s (u p d)").bitcast(F32)
+                for u in range(2):
+                    nc.tensor.transpose(h_turned[:, st, u, :], h_words[:, u * P : (u + 1) * P], ident[:])
+            h_bf = work.tile([P, C * PACK], BF16, name="h_bf", align_bytes=64)
+            nc.scalar.copy(
+                out=h_bf[:].bitcast(F32).rearrange("p (t s u) -> p t s u", t=2, u=2),
+                in_=h_turned[:].rearrange("p t u s -> p t s u"),
+            )
+            h_codes = work.tile([P, C], U32, name="h_codes", align_bytes=64)
+            h_scales = work.tile([P, C], U8, name="h_scales", align_bytes=64)
+            nc.vector.quantize_mx(out=h_codes[:].bitcast(FP8X4), scales=h_scales[:], in_=h_bf[:])
+            for r0, nr in ((0, 2), (2, 1)):
+                y = psum.tile([P, nr, C], F32, name="y")
+                for r in range(r0, r0 + nr):
+                    nc.tensor.matmul_mx(
+                        out=y[:, r - r0, :],
+                        lhsT=w2[pair][:, side, 2 * P * r : 2 * P * (r + 1)].bitcast(FP4X4),
+                        lhsT_scale=s2[:, e, P * r : P * (r + 1)],
+                        rhs=h_codes[:].bitcast(FP8X4),
+                        rhs_scale=h_scales[:],
+                        start=True,
+                        stop=True,
+                    )
+                nc.scalar.copy(out=y_pairs[pair][:, r0 : r0 + nr, side, :], in_=y[:])
+
+        for r in range(ROW_BLOCKS):
+            window = keep.tile([P, S], F32, name="window%d" % r)
+            for pair in range(PAIRS):
+                half, c0 = divmod(pair * 2 * C, S // 2)
+                nc.vector.tensor_tensor(
+                    window[:].indirect(offsets[:, pair * (2 * C // 16) : (pair + 1) * (2 * C // 16)]),
+                    y_pairs[pair][:, r, :, :].rearrange("p a c -> p (a c)"),
+                    gates[r, half][:, c0 : c0 + 2 * C],
+                    MULT,
+                )
+            nc.sync.dma_start(out=out[r * P : (r + 1) * P, : T // 2], in_=window[:, : T // 2])
+            nc.scalar.dma_start(out=out[r * P : (r + 1) * P, T // 2 :], in_=window[:, T // 2 : T])

@@ -7,6 +7,8 @@ K, T, E, C, H, N = 512, 1280, 8, 256, 512, 384
 S = E * C
 P = 128
 PACK = 4
+PAIRS = E // 2
+LIST_COLS = C // 16
 FLOPS = 2 * S * (2 * K * H + H * N)
 
 F32 = mybir.dt.float32
@@ -19,10 +21,14 @@ FP8X4 = mybir.dt.float8_e4m3fn_x4
 FP4X4 = mybir.dt.float4_e2m1fn_x4
 MULT = mybir.AluOpType.mult
 RELU = mybir.ActivationFunctionType.Relu
+COPY = mybir.ActivationFunctionType.Copy
 
-X_CHUNKS = (256, 256, 256, 256, 128, 128)
-ROW_BLOCKS = N // P
-PAIRS = E // 2
+X_CHUNKS = ((512,), (256, 128), (256,), (128,))
+GATHERS = ((0, 1), (1, 1), (2, 2), (4, 4))
+HELD_BEHIND = 1
+TURN_LAG, SECOND_LAG = 1, 3
+BANKS_A, BANKS_B, BANKS_TURNED, BANKS_Y = 2, 3, 2, 1
+TILE_BUFS, EXPERT_BUFS = 8, 4
 
 
 def tile_moe_pad_glu_relu_kernel(
@@ -31,137 +37,212 @@ def tile_moe_pad_glu_relu_kernel(
     nc = tc.nc
     with ExitStack() as ctx:
         keep = ctx.enter_context(tc.tile_pool(name="keep", bufs=1))
-        work = ctx.enter_context(tc.tile_pool(name="work", bufs=3))
+        per_expert = ctx.enter_context(tc.tile_pool(name="per_expert", bufs=EXPERT_BUFS))
+        per_tile = ctx.enter_context(tc.tile_pool(name="per_tile", bufs=TILE_BUFS))
         psum = ctx.enter_context(tc.psum_pool(name="psum", bufs=2))
 
         offsets = keep.tile([P, S // 16], U16, name="offsets")
-        x_raw = [keep.tile([P, PACK, w], F32, name="x_raw%d" % i) for i, w in enumerate(X_CHUNKS)]
-        starts = [sum(X_CHUNKS[:i]) for i in range(len(X_CHUNKS))]
-        x_rows = xT.rearrange("(p j) t -> p j t", j=PACK)
-        for raw, t0, w in zip(x_raw, starts, X_CHUNKS):
-            nc.sync.dma_start(out=raw[:], in_=x_rows[:, :, t0 : t0 + w])
-        nc.sync.dma_start(offsets[:], offs)
+        widths = [sum(parts) for parts in X_CHUNKS]
+        starts = [sum(widths[:i]) for i in range(len(widths))]
+        x_raw = [keep.tile([P, PACK, w], F32, name="x_raw%d" % i) for i, w in enumerate(widths)]
 
-        tok_words = keep.tile([P, S], I32, name="tok_words", align_bytes=64)
-        tok_scales = keep.tile([P, S], U8, name="tok_scales", align_bytes=64)
-        nc.gpsimd.memset(tok_scales[:], 0)
-        nc.vector.memset(tok_words[:, T:], 0)
-        ident = keep.tile([P, P], F32, name="ident")
-        make_identity(nc, ident[:])
+        def expert_offsets(first, count):
+            return offsets[:, first * LIST_COLS : (first + count) * LIST_COLS]
 
         def scale_plane(name, width):
             plane = keep.tile([P, E, width], U8, name=name, align_bytes=64)
             nc.vector.memset(plane[:].bitcast(I32), 0)
             return plane
 
-        def load_plane(plane, scales):
-            for q in range(4):
-                nc.sync.dma_start(
-                    out=plane[32 * q : 32 * q + 4, :, :].bitcast(I32),
-                    in_=scales[:, 0, 4 * q : 4 * q + 4, :].rearrange("e r n -> r e n").bitcast(I32),
-                )
+        def load_scale_rows(plane, scales, quadrant):
+            rows = scales[:, 0, 4 * quadrant : 4 * quadrant + 4, :]
+            nc.sync.dma_start(
+                out=plane[32 * quadrant : 32 * quadrant + 4, :, :].bitcast(I32),
+                in_=rows.rearrange("e r n -> r e n").bitcast(I32),
+            )
 
         def load_words(name, words, pair):
-            width = words.shape[3]
-            tile = keep.tile([P, 2, width], U8, name="%s_%d" % (name, pair), align_bytes=64)
+            tile = keep.tile([P, 2, words.shape[3]], U8, name="%s_%d" % (name, pair), align_bytes=64)
             nc.sync.dma_start(
                 out=tile[:].bitcast(I32),
                 in_=words[2 * pair : 2 * pair + 2, 0].rearrange("e p n -> p e n").bitcast(I32),
             )
             return tile
 
+        def load_gate_rows(pair):
+            tile = keep.tile([P, 2, 2 * C], F32, name="gate01_%d" % pair)
+            nc.sync.dma_start(
+                out=tile[:],
+                in_=gate[: 2 * P, pair * 2 * C : (pair + 1) * 2 * C].rearrange("(r p) c -> p r c", p=P),
+            )
+            return tile
+
         s1 = scale_plane("s1", H)
         s3 = scale_plane("s3", H)
+        tok_words = keep.tile([P, S], I32, name="tok_words", align_bytes=64)
+        tok_scales = keep.tile([P, S], U8, name="tok_scales", align_bytes=64)
+        nc.vector.memset(tok_scales[:].bitcast(I32), 0)
+        nc.vector.memset(tok_words[:, T:], 0)
         s2 = scale_plane("s2", N)
-        load_plane(s1, w1_scales)
-        load_plane(s3, w3_scales)
-        load_plane(s2, w2_scales)
-        w1, w3, w2, gates = [], [], [], {}
+        ident = keep.tile([P, P], F32, name="ident")
+        ident_made = keep.tile([P, P], F32, name="ident_made")
+        make_identity(nc, ident_made[:])
+        nc.scalar.activation(ident[:], ident_made[:], RELU)
+
+        x_rows = xT.rearrange("(p j) t -> p j t", j=PACK)
+        for raw, t0, w in zip(x_raw, starts, widths):
+            nc.sync.dma_start(out=raw[:], in_=x_rows[:, :, t0 : t0 + w])
+        nc.sync.dma_start(offsets[:], offs)
+        w3 = [load_words("w3", w3_words, 0)]
+        w1 = [load_words("w1", w1_words, 0)]
+        for quadrant in range(4):
+            load_scale_rows(s1, w1_scales, quadrant)
+            load_scale_rows(s3, w3_scales, quadrant)
+        w2, gate01 = [], []
         for pair in range(PAIRS):
-            w1.append(load_words("w1", w1_words, pair))
-            w3.append(load_words("w3", w3_words, pair))
+            if pair + 1 < PAIRS:
+                w1.append(load_words("w1", w1_words, pair + 1))
+                w3.append(load_words("w3", w3_words, pair + 1))
+            if pair == 0:
+                for quadrant in range(4):
+                    load_scale_rows(s2, w2_scales, quadrant)
             w2.append(load_words("w2", w2_words, pair))
-        for r in range(ROW_BLOCKS):
-            for half in range(2):
-                g = keep.tile([P, S // 2], F32, name="gate_%d_%d" % (r, half))
-                nc.sync.dma_start(
-                    out=g[:], in_=gate[r * P : (r + 1) * P, half * (S // 2) : (half + 1) * (S // 2)]
-                )
-                gates[r, half] = g
+            gate01.append(load_gate_rows(pair))
+        gate2 = keep.tile([P, S], F32, name="gate2")
+        nc.sync.dma_start(out=gate2[:], in_=gate[2 * P :, :])
 
-        for i, (raw, t0, w) in enumerate(zip(x_raw, starts, X_CHUNKS)):
+        for i, (raw, t0, w) in enumerate(zip(x_raw, starts, widths)):
             x_bf = keep.tile([P, w, PACK], BF16, name="x_bf%d" % i, align_bytes=64)
-            nc.vector.tensor_copy(out=x_bf[:], in_=raw[:].rearrange("p j t -> p t j"))
-            nc.vector.quantize_mx(
-                out=tok_words[:, t0 : t0 + w].bitcast(FP8X4),
-                scales=tok_scales[:, t0 : t0 + w],
-                in_=x_bf[:].rearrange("p t j -> p (t j)"),
-            )
-
-        y_pairs = [keep.tile([P, ROW_BLOCKS, 2, C], F32, name="y_%d" % i) for i in range(PAIRS)]
-        for e in range(E):
-            pair, side = divmod(e, 2)
-            slot_offsets = offsets[:, e * (C // 16) : (e + 1) * (C // 16)]
-            slot_words = keep.tile([P, C], U32, name="slot_words%d" % e, align_bytes=64)
-            slot_scales = keep.tile([P, C], U8, name="slot_scales%d" % e, align_bytes=64)
-            nc.vector.tensor_copy(slot_words[:], tok_words[:].bitcast(U32).indirect(slot_offsets))
-            nc.vector.tensor_copy(slot_scales[:], tok_scales[:].indirect(slot_offsets))
-
-            h_turned = psum.tile([P, 2, 2, P], F32, name="h_turned")
-            for st in range(2):
-                cols = slice(st * P, (st + 1) * P)
-                a = psum.tile([P, H], F32, name="a")
-                b = psum.tile([P, H], F32, name="b")
-                for acc, w, s in ((a, w1, s1), (b, w3, s3)):
-                    nc.tensor.matmul_mx(
-                        out=acc[:],
-                        lhsT=slot_words[:, cols].bitcast(FP8X4),
-                        lhsT_scale=slot_scales[:, cols],
-                        rhs=w[pair][:, side, :].bitcast(FP4X4),
-                        rhs_scale=s[:, e, :],
-                        start=True,
-                        stop=True,
-                    )
-                relu_a = work.tile([P, 2, P, 2], F32, name="relu_a")
-                nc.scalar.activation(relu_a[:], a[:].rearrange("s (p u d) -> s u p d", u=2, d=2), RELU)
-                h = work.tile([P, 2, P, 2], BF16, name="h")
-                nc.vector.tensor_tensor(
-                    h[:], b[:].rearrange("s (p u d) -> s u p d", u=2, d=2), relu_a[:], MULT
+            half = w // 2
+            nc.scalar.activation(x_bf[:, half:, :], raw[:, :, half:].rearrange("p j t -> p t j"), COPY)
+            nc.vector.tensor_copy(out=x_bf[:, :half, :], in_=raw[:, :, :half].rearrange("p j t -> p t j"))
+            done = 0
+            for part in X_CHUNKS[i]:
+                tokens = slice(t0 + done, t0 + done + part)
+                nc.vector.quantize_mx(
+                    out=tok_words[:, tokens].bitcast(FP8X4),
+                    scales=tok_scales[:, tokens],
+                    in_=x_bf[:, done : done + part, :].rearrange("p t j -> p (t j)"),
                 )
-                h_words = h[:].rearrange("s u p d -> s (u p d)").bitcast(F32)
-                for u in range(2):
-                    nc.tensor.transpose(h_turned[:, st, u, :], h_words[:, u * P : (u + 1) * P], ident[:])
-            h_bf = work.tile([P, C * PACK], BF16, name="h_bf", align_bytes=64)
+                done += part
+
+        slot_words, slot_scales = {}, {}
+
+        def gather_words(first, count, tag):
+            tile = keep.tile([P, count * C], U32, name="slot_words%d" % first, tag=tag, align_bytes=64)
+            nc.vector.tensor_copy(tile[:], tok_words[:].bitcast(U32).indirect(expert_offsets(first, count)))
+            for i in range(count):
+                slot_words[first + i] = tile[:, i * C : (i + 1) * C]
+
+        def gather_scales(first, count):
+            tile = keep.tile([P, count * C], U8, name="slot_scales%d" % first, align_bytes=64)
+            nc.vector.tensor_copy(tile[:], tok_scales[:].indirect(expert_offsets(first, count)))
+            for i in range(count):
+                slot_scales[first + i] = tile[:, i * C : (i + 1) * C]
+
+        for first, count in GATHERS[:-1]:
+            gather_words(first, count, "slot_words%d" % first)
+            gather_scales(first, count)
+        gather_scales(*GATHERS[-1])
+
+        y2 = keep.tile([P, S], F32, name="y2")
+        y01 = [keep.tile([P, 2, 2 * C], F32, name="y01_%d" % pair) for pair in range(PAIRS)]
+        windows = [keep.tile([P, S], F32, name="window%d" % r) for r in range(2)]
+        h_tiles, h_quant = {}, {}
+
+        def first_layer(e, tile):
+            pair, side = divmod(e, 2)
+            slots = slice(tile * P, (tile + 1) * P)
+            a = psum.tile([P, H], F32, name="a", bufs=BANKS_A)
+            b = psum.tile([P, H], F32, name="b", bufs=BANKS_B)
+            for acc, words, plane in ((a, w1, s1), (b, w3, s3)):
+                nc.tensor.matmul_mx(
+                    out=acc[:],
+                    lhsT=slot_words[e][:, slots].bitcast(FP8X4),
+                    lhsT_scale=slot_scales[e][:, slots],
+                    rhs=words[pair][:, side, :].bitcast(FP4X4),
+                    rhs_scale=plane[:, e, :],
+                    start=True,
+                    stop=True,
+                )
+            holds_gather = (e, tile) == (HELD_BEHIND, 0)
+            if holds_gather:
+                relu_a = keep.tile([P, H], F32, name="relu_a_held", tag="held", align_bytes=64)
+            else:
+                relu_a = per_tile.tile([P, H], F32, name="relu_a")
+            nc.scalar.activation(relu_a[:], a[:], RELU)
+            h = per_tile.tile([P, H], BF16, name="h")
+            nc.vector.tensor_tensor(h[:], relu_a[:], b[:], MULT)
+            h_tiles[e, tile] = h
+            if holds_gather:
+                gather_words(*GATHERS[-1], "held")
+
+        def turn_and_quantise(e):
+            h_turned = psum.tile([P, 2, 2, P], F32, name="h_turned", bufs=BANKS_TURNED)
+            h_bf = per_expert.tile([P, C * PACK], BF16, name="h_bf", align_bytes=64)
+            for tile in range(2):
+                pairs_of_i = h_tiles[e, tile][:].bitcast(F32)
+                for parity in range(2):
+                    nc.tensor.transpose(h_turned[:, tile, parity, :], pairs_of_i[:, parity::2], ident[:])
             nc.scalar.copy(
                 out=h_bf[:].bitcast(F32).rearrange("p (t s u) -> p t s u", t=2, u=2),
                 in_=h_turned[:].rearrange("p t u s -> p t s u"),
             )
-            h_codes = work.tile([P, C], U32, name="h_codes", align_bytes=64)
-            h_scales = work.tile([P, C], U8, name="h_scales", align_bytes=64)
-            nc.vector.quantize_mx(out=h_codes[:].bitcast(FP8X4), scales=h_scales[:], in_=h_bf[:])
-            for r0, nr in ((0, 2), (2, 1)):
-                y = psum.tile([P, nr, C], F32, name="y")
-                for r in range(r0, r0 + nr):
-                    nc.tensor.matmul_mx(
-                        out=y[:, r - r0, :],
-                        lhsT=w2[pair][:, side, 2 * P * r : 2 * P * (r + 1)].bitcast(FP4X4),
-                        lhsT_scale=s2[:, e, P * r : P * (r + 1)],
-                        rhs=h_codes[:].bitcast(FP8X4),
-                        rhs_scale=h_scales[:],
-                        start=True,
-                        stop=True,
-                    )
-                nc.scalar.copy(out=y_pairs[pair][:, r0 : r0 + nr, side, :], in_=y[:])
+            h_words = keep.tile([P, C], U32, name="h_words%d" % e, align_bytes=64)
+            h_scales = keep.tile([P, C], U8, name="h_scales%d" % e, align_bytes=64)
+            nc.vector.quantize_mx(out=h_words[:].bitcast(FP8X4), scales=h_scales[:], in_=h_bf[:])
+            h_quant[e] = (h_words, h_scales)
 
-        for r in range(ROW_BLOCKS):
-            window = keep.tile([P, S], F32, name="window%d" % r)
-            for pair in range(PAIRS):
-                half, c0 = divmod(pair * 2 * C, S // 2)
+        def project(acc, e, r):
+            pair, side = divmod(e, 2)
+            h_words, h_scales = h_quant[e]
+            nc.tensor.matmul_mx(
+                out=acc,
+                lhsT=w2[pair][:, side, 2 * P * r : 2 * P * (r + 1)].bitcast(FP4X4),
+                lhsT_scale=s2[:, e, P * r : P * (r + 1)],
+                rhs=h_words[:].bitcast(FP8X4),
+                rhs_scale=h_scales[:],
+                start=True,
+                stop=True,
+            )
+
+        def second_layer(e):
+            pair, side = divmod(e, 2)
+            y = psum.tile([P, 2, C], F32, name="y", bufs=BANKS_Y)
+            for r in range(2):
+                project(y[:, r, :], e, r)
+            nc.scalar.copy(out=y01[pair][:, :, side * C : (side + 1) * C], in_=y[:])
+
+        for step in range(E + SECOND_LAG):
+            if step < E:
+                first_layer(step, 0)
+                first_layer(step, 1)
+            if 0 <= step - TURN_LAG < E:
+                turn_and_quantise(step - TURN_LAG)
+            if 0 <= step - SECOND_LAG < E:
+                second_layer(step - SECOND_LAG)
+
+        for pair in range(PAIRS):
+            y = psum.tile([P, 2, C], F32, name="y", bufs=BANKS_Y)
+            for side in range(2):
+                project(y[:, side, :], 2 * pair + side, 2)
+            nc.scalar.copy(
+                out=y2[:, pair * 2 * C : (pair + 1) * 2 * C], in_=y[:].rearrange("p a c -> p (a c)")
+            )
+
+        for e in range(E):
+            pair, side = divmod(e, 2)
+            slots = slice(side * C, (side + 1) * C)
+            for r in range(2):
                 nc.vector.tensor_tensor(
-                    window[:].indirect(offsets[:, pair * (2 * C // 16) : (pair + 1) * (2 * C // 16)]),
-                    y_pairs[pair][:, r, :, :].rearrange("p a c -> p (a c)"),
-                    gates[r, half][:, c0 : c0 + 2 * C],
+                    windows[r][:].indirect(expert_offsets(e, 1)),
+                    y01[pair][:, r, slots],
+                    gate01[pair][:, r, slots],
                     MULT,
                 )
-            nc.sync.dma_start(out=out[r * P : (r + 1) * P, : T // 2], in_=window[:, : T // 2])
-            nc.scalar.dma_start(out=out[r * P : (r + 1) * P, T // 2 :], in_=window[:, T // 2 : T])
+        for r in range(2):
+            nc.sync.dma_start(out=out[r * P : (r + 1) * P, :], in_=windows[r][:, :T])
+        window2 = keep.tile([P, 2 * S], F32, name="window2")
+        nc.vector.tensor_tensor(window2[:].indirect(offsets[:]), y2[:], gate2[:], MULT)
+        nc.sync.dma_start(out=out[2 * P :, : T // 2], in_=window2[:, : T // 2])
+        nc.scalar.dma_start(out=out[2 * P :, T // 2 :], in_=window2[:, T // 2 : T])

from contextlib import ExitStack

import concourse.mybir as mybir
from concourse.masks import make_identity

K, T, E, C, H, N = 512, 1280, 8, 256, 512, 384
S = E * C
P = 128
PACK = 4
PAIRS = E // 2
LIST_COLS = C // 16
FLOPS = 2 * S * (2 * K * H + H * N)

F32 = mybir.dt.float32
BF16 = mybir.dt.bfloat16
I32 = mybir.dt.int32
U32 = mybir.dt.uint32
U16 = mybir.dt.uint16
U8 = mybir.dt.uint8
FP8X4 = mybir.dt.float8_e4m3fn_x4
FP4X4 = mybir.dt.float4_e2m1fn_x4
MULT = mybir.AluOpType.mult
RELU = mybir.ActivationFunctionType.Relu
COPY = mybir.ActivationFunctionType.Copy

X_CHUNKS = ((512,), (256, 128), (256,), (128,))
GATHERS = ((0, 1), (1, 1), (2, 2), (4, 4))
HELD_BEHIND = 1
TURN_LAG, SECOND_LAG = 1, 3
BANKS_A, BANKS_B, BANKS_TURNED, BANKS_Y = 2, 3, 2, 1
TILE_BUFS, EXPERT_BUFS = 8, 4


def tile_moe_pad_glu_relu_kernel(
    tc, xT, w1_words, w1_scales, w3_words, w3_scales, w2_words, w2_scales, gate, offs, out
):
    nc = tc.nc
    with ExitStack() as ctx:
        keep = ctx.enter_context(tc.tile_pool(name="keep", bufs=1))
        per_expert = ctx.enter_context(tc.tile_pool(name="per_expert", bufs=EXPERT_BUFS))
        per_tile = ctx.enter_context(tc.tile_pool(name="per_tile", bufs=TILE_BUFS))
        psum = ctx.enter_context(tc.psum_pool(name="psum", bufs=2))

        offsets = keep.tile([P, S // 16], U16, name="offsets")
        widths = [sum(parts) for parts in X_CHUNKS]
        starts = [sum(widths[:i]) for i in range(len(widths))]
        x_raw = [keep.tile([P, PACK, w], F32, name="x_raw%d" % i) for i, w in enumerate(widths)]

        def expert_offsets(first, count):
            return offsets[:, first * LIST_COLS : (first + count) * LIST_COLS]

        def scale_plane(name, width):
            plane = keep.tile([P, E, width], U8, name=name, align_bytes=64)
            nc.vector.memset(plane[:].bitcast(I32), 0)
            return plane

        def load_scale_rows(plane, scales, quadrant):
            rows = scales[:, 0, 4 * quadrant : 4 * quadrant + 4, :]
            nc.sync.dma_start(
                out=plane[32 * quadrant : 32 * quadrant + 4, :, :].bitcast(I32),
                in_=rows.rearrange("e r n -> r e n").bitcast(I32),
            )

        def load_words(name, words, pair):
            tile = keep.tile([P, 2, words.shape[3]], U8, name="%s_%d" % (name, pair), align_bytes=64)
            nc.sync.dma_start(
                out=tile[:].bitcast(I32),
                in_=words[2 * pair : 2 * pair + 2, 0].rearrange("e p n -> p e n").bitcast(I32),
            )
            return tile

        def load_gate_rows(pair):
            tile = keep.tile([P, 2, 2 * C], F32, name="gate01_%d" % pair)
            nc.sync.dma_start(
                out=tile[:],
                in_=gate[: 2 * P, pair * 2 * C : (pair + 1) * 2 * C].rearrange("(r p) c -> p r c", p=P),
            )
            return tile

        s1 = scale_plane("s1", H)
        s3 = scale_plane("s3", H)
        tok_words = keep.tile([P, S], I32, name="tok_words", align_bytes=64)
        tok_scales = keep.tile([P, S], U8, name="tok_scales", align_bytes=64)
        nc.vector.memset(tok_scales[:].bitcast(I32), 0)
        nc.vector.memset(tok_words[:, T:], 0)
        s2 = scale_plane("s2", N)
        ident = keep.tile([P, P], F32, name="ident")
        ident_made = keep.tile([P, P], F32, name="ident_made")
        make_identity(nc, ident_made[:])
        nc.scalar.activation(ident[:], ident_made[:], RELU)

        x_rows = xT.rearrange("(p j) t -> p j t", j=PACK)
        for raw, t0, w in zip(x_raw, starts, widths):
            nc.sync.dma_start(out=raw[:], in_=x_rows[:, :, t0 : t0 + w])
        nc.sync.dma_start(offsets[:], offs)
        w3 = [load_words("w3", w3_words, 0)]
        w1 = [load_words("w1", w1_words, 0)]
        for quadrant in range(4):
            load_scale_rows(s1, w1_scales, quadrant)
            load_scale_rows(s3, w3_scales, quadrant)
        w2, gate01 = [], []
        for pair in range(PAIRS):
            if pair + 1 < PAIRS:
                w1.append(load_words("w1", w1_words, pair + 1))
                w3.append(load_words("w3", w3_words, pair + 1))
            if pair == 0:
                for quadrant in range(4):
                    load_scale_rows(s2, w2_scales, quadrant)
            w2.append(load_words("w2", w2_words, pair))
            gate01.append(load_gate_rows(pair))
        gate2 = keep.tile([P, S], F32, name="gate2")
        nc.sync.dma_start(out=gate2[:], in_=gate[2 * P :, :])

        for i, (raw, t0, w) in enumerate(zip(x_raw, starts, widths)):
            x_bf = keep.tile([P, w, PACK], BF16, name="x_bf%d" % i, align_bytes=64)
            half = w // 2
            nc.scalar.activation(x_bf[:, half:, :], raw[:, :, half:].rearrange("p j t -> p t j"), COPY)
            nc.vector.tensor_copy(out=x_bf[:, :half, :], in_=raw[:, :, :half].rearrange("p j t -> p t j"))
            done = 0
            for part in X_CHUNKS[i]:
                tokens = slice(t0 + done, t0 + done + part)
                nc.vector.quantize_mx(
                    out=tok_words[:, tokens].bitcast(FP8X4),
                    scales=tok_scales[:, tokens],
                    in_=x_bf[:, done : done + part, :].rearrange("p t j -> p (t j)"),
                )
                done += part

        slot_words, slot_scales = {}, {}

        def gather_words(first, count, tag):
            tile = keep.tile([P, count * C], U32, name="slot_words%d" % first, tag=tag, align_bytes=64)
            nc.vector.tensor_copy(tile[:], tok_words[:].bitcast(U32).indirect(expert_offsets(first, count)))
            for i in range(count):
                slot_words[first + i] = tile[:, i * C : (i + 1) * C]

        def gather_scales(first, count):
            tile = keep.tile([P, count * C], U8, name="slot_scales%d" % first, align_bytes=64)
            nc.vector.tensor_copy(tile[:], tok_scales[:].indirect(expert_offsets(first, count)))
            for i in range(count):
                slot_scales[first + i] = tile[:, i * C : (i + 1) * C]

        for first, count in GATHERS[:-1]:
            gather_words(first, count, "slot_words%d" % first)
            gather_scales(first, count)
        gather_scales(*GATHERS[-1])

        y2 = keep.tile([P, S], F32, name="y2")
        y01 = [keep.tile([P, 2, 2 * C], F32, name="y01_%d" % pair) for pair in range(PAIRS)]
        windows = [keep.tile([P, S], F32, name="window%d" % r) for r in range(2)]
        h_tiles, h_quant = {}, {}

        def first_layer(e, tile):
            pair, side = divmod(e, 2)
            slots = slice(tile * P, (tile + 1) * P)
            a = psum.tile([P, H], F32, name="a", bufs=BANKS_A)
            b = psum.tile([P, H], F32, name="b", bufs=BANKS_B)
            for acc, words, plane in ((a, w1, s1), (b, w3, s3)):
                nc.tensor.matmul_mx(
                    out=acc[:],
                    lhsT=slot_words[e][:, slots].bitcast(FP8X4),
                    lhsT_scale=slot_scales[e][:, slots],
                    rhs=words[pair][:, side, :].bitcast(FP4X4),
                    rhs_scale=plane[:, e, :],
                    start=True,
                    stop=True,
                )
            holds_gather = (e, tile) == (HELD_BEHIND, 0)
            if holds_gather:
                relu_a = keep.tile([P, H], F32, name="relu_a_held", tag="held", align_bytes=64)
            else:
                relu_a = per_tile.tile([P, H], F32, name="relu_a")
            nc.scalar.activation(relu_a[:], a[:], RELU)
            h = per_tile.tile([P, H], BF16, name="h")
            nc.vector.tensor_tensor(h[:], relu_a[:], b[:], MULT)
            h_tiles[e, tile] = h
            if holds_gather:
                gather_words(*GATHERS[-1], "held")

        def turn_and_quantise(e):
            h_turned = psum.tile([P, 2, 2, P], F32, name="h_turned", bufs=BANKS_TURNED)
            h_bf = per_expert.tile([P, C * PACK], BF16, name="h_bf", align_bytes=64)
            for tile in range(2):
                pairs_of_i = h_tiles[e, tile][:].bitcast(F32)
                for parity in range(2):
                    nc.tensor.transpose(h_turned[:, tile, parity, :], pairs_of_i[:, parity::2], ident[:])
            nc.scalar.copy(
                out=h_bf[:].bitcast(F32).rearrange("p (t s u) -> p t s u", t=2, u=2),
                in_=h_turned[:].rearrange("p t u s -> p t s u"),
            )
            h_words = keep.tile([P, C], U32, name="h_words%d" % e, align_bytes=64)
            h_scales = keep.tile([P, C], U8, name="h_scales%d" % e, align_bytes=64)
            nc.vector.quantize_mx(out=h_words[:].bitcast(FP8X4), scales=h_scales[:], in_=h_bf[:])
            h_quant[e] = (h_words, h_scales)

        def project(acc, e, r):
            pair, side = divmod(e, 2)
            h_words, h_scales = h_quant[e]
            nc.tensor.matmul_mx(
                out=acc,
                lhsT=w2[pair][:, side, 2 * P * r : 2 * P * (r + 1)].bitcast(FP4X4),
                lhsT_scale=s2[:, e, P * r : P * (r + 1)],
                rhs=h_words[:].bitcast(FP8X4),
                rhs_scale=h_scales[:],
                start=True,
                stop=True,
            )

        def second_layer(e):
            pair, side = divmod(e, 2)
            y = psum.tile([P, 2, C], F32, name="y", bufs=BANKS_Y)
            for r in range(2):
                project(y[:, r, :], e, r)
            nc.scalar.copy(out=y01[pair][:, :, side * C : (side + 1) * C], in_=y[:])

        for step in range(E + SECOND_LAG):
            if step < E:
                first_layer(step, 0)
                first_layer(step, 1)
            if 0 <= step - TURN_LAG < E:
                turn_and_quantise(step - TURN_LAG)
            if 0 <= step - SECOND_LAG < E:
                second_layer(step - SECOND_LAG)

        for pair in range(PAIRS):
            y = psum.tile([P, 2, C], F32, name="y", bufs=BANKS_Y)
            for side in range(2):
                project(y[:, side, :], 2 * pair + side, 2)
            nc.scalar.copy(
                out=y2[:, pair * 2 * C : (pair + 1) * 2 * C], in_=y[:].rearrange("p a c -> p (a c)")
            )

        for e in range(E):
            pair, side = divmod(e, 2)
            slots = slice(side * C, (side + 1) * C)
            for r in range(2):
                nc.vector.tensor_tensor(
                    windows[r][:].indirect(expert_offsets(e, 1)),
                    y01[pair][:, r, slots],
                    gate01[pair][:, r, slots],
                    MULT,
                )
        for r in range(2):
            nc.sync.dma_start(out=out[r * P : (r + 1) * P, :], in_=windows[r][:, :T])
        window2 = keep.tile([P, 2 * S], F32, name="window2")
        nc.vector.tensor_tensor(window2[:].indirect(offsets[:]), y2[:], gate2[:], MULT)
        nc.sync.dma_start(out=out[2 * P :, : T // 2], in_=window2[:, : T // 2])
        nc.scalar.dma_start(out=out[2 * P :, T // 2 :], in_=window2[:, T // 2 : T])
